import numpy as np, ml_dtypes
CORES = [2,42,66,74,82,90,114]
N = 7
import mx_ref
NC, WT = 512, 1
BF = ml_dtypes.bfloat16
def setup_inputs(rng):
    def f(*shape):
        return mx_ref.flush((rng.standard_normal(shape, dtype=np.float32) * np.exp2(rng.integers(-2, 3, shape[:-1] + (1,)))).astype(BF))
    return {"w": f(N, 128, WT * 512), "x": f(N, 128, 4 * NC)}
def setup_inputs_blocks(rng):
    d = setup_inputs(rng)
    for k in ("w", "x"): d[k] = mx_ref.spread(d[k], rng, 4)
    return d
def setup_inputs_wide(rng):
    d = setup_inputs(rng)
    for k in ("w", "x"): d[k] = mx_ref.flush((d[k].astype(np.float32) * np.exp2(rng.integers(-8, 9, (N, 1, 1))).astype(np.float32)).astype(BF))
    return d
def setup_inputs_zeros(rng):
    d = setup_inputs(rng); v = d["x"].reshape(N, 128, -1, 4).copy()
    v[np.broadcast_to((rng.random((N, 1, v.shape[2], 1)) < 0.33), v.shape)] = 0
    d["x"] = v.reshape(d["x"].shape)
    return d
def reference(w, x):
    QW = [mx_ref.quantize(w[b // WT][:, 512 * (b % WT):512 * (b % WT) + 512]) for b in range(N * WT)]
    y = np.zeros((N, 128, N * WT * NC), np.float32)
    for r in range(N):
        qx = mx_ref.quantize(x[r])
        for b in range(N * WT):
            y[r][:, NC * b:NC * b + NC] = mx_ref.matmul(QW[b], qx)
    return {"y": y}

from concourse.bass import DstId, RemoteDMATransfer
from concourse.mybir import dt, ActivationFunctionType

N = 7
WC = 128
NC = 512

DIRECT = (2, 4, 6)
RELAYED = (1, 3, 5)

SCRATCH = {
    "wt": ("sbuf", [128, 4 * WC], "bfloat16"),
    "xt": ("sbuf", [128, 4 * NC], "bfloat16"),
    "qw": ("sbuf", [128, N * WC], "float8_e4m3fn_x4"),
    "sw": ("sbuf", [128, N * WC], "uint8"),
    "qx": ("sbuf", [128, NC], "float8_e4m3fn_x4"),
    "sx": ("sbuf", [128, NC], "uint8"),
    "ps": ("psum", [128, N * NC], "float32"),
    "ys": ("sbuf", [128, N * NC], "float32"),
}
SEMAPHORES = (["ldw", "ldx", "qwd", "qxd", "sent", "stored", "relp", "relc"]
              + ["arr%d" % b for b in range(N)] + ["mm%d" % b for b in range(N)] + ["cp%d" % b for b in range(N)])


def _engines(mask):
    return bin(mask).count("1")


def _relay_of(j, cores, topo):
    src = cores[j]
    dests = [cores[(j + k) % N] for k in RELAYED]
    for c in range(topo.CHIPS * topo.CORES_PER_CHIP):
        if (topo.chip(c) == topo.chip(src) and topo.die(c) != topo.die(src) and c not in cores
                and all(topo.may_write(c, d) for d in dests)):
            return c
    return None


def rank_program(g, core, T, topo):
    cores = list(T.cores)
    sem = T.sem

    def codes(b):
        return T.qw[:, WC * b:WC * (b + 1)].bitcast(dt.uint8)

    def plane(b):
        return T.sw[:, WC * b:WC * (b + 1)]

    def put(dst, b, part):
        rid, pid, _ = topo.addr(dst)
        mask = topo.mask(core, dst)
        g.remote_dma(part(b), part(b), sem["arr%d" % b], sem.sent, pid, rid, mask)
        return _engines(mask)

    rank = T.rank_of(core)

    if rank is None:
        for j in range(N):
            if _relay_of(j, cores, topo) != core:
                continue
            got = _engines(topo.mask(cores[j], core) & ~topo.mask(cores[j], cores[(j + DIRECT[0]) % N]))
            sent = 0
            for i, k in enumerate(RELAYED):
                dst = cores[(j + k) % N]
                if i == 0:
                    g.wait_ge(sem.relp, got)
                sent += put(dst, j, plane)
                if i == 0:
                    g.wait_ge(sem.relc, got)
                sent += put(dst, j, codes)
            g.wait_ge(sem.sent, sent)
        return

    def blk(b):
        return slice(NC * b, NC * (b + 1))

    g.sync.dma_start(T.wt[:], T.w[:]).then_inc(sem.ldw, 16)
    g.sync.dma_start(T.xt[:], T.x[:]).then_inc(sem.ldx, 16)

    g.vector.wait_ge(sem.ldw, 16)
    g.vector.quantize_mx(T.qw[:, WC * rank:WC * (rank + 1)], plane(rank), T.wt[:]).then_inc(sem.qwd, 1)
    g.vector.wait_ge(sem.ldx, 16)
    g.vector.quantize_mx(T.qx[:], T.sx[:], T.xt[:]).then_inc(sem.qxd, 1)

    relay = _relay_of(rank, cores, topo)
    first = cores[(rank + DIRECT[0]) % N]
    off = topo.mask(core, first)
    on = topo.mask(core, relay) & ~off
    f_rid, f_pid, _ = topo.addr(first)
    r_rid, r_pid, _ = topo.addr(relay)
    g.wait_ge(sem.qwd, 1)
    sent = 0
    for part, rsem in ((plane, sem.relp), (codes, sem.relc)):
        g.remote_dma_fused([
            RemoteDMATransfer(dst_ids=[DstId(rid=r_rid, pnc=r_pid)], dma_engine_mask=on, remote_sem=rsem,
                              src=part(rank), dst=part(rank)),
            RemoteDMATransfer(dst_ids=[DstId(rid=f_rid, pnc=f_pid)], dma_engine_mask=off,
                              remote_sem=sem["arr%d" % rank], src=part(rank), dst=part(rank)),
        ], local_sem=sem.sent)
        sent += _engines(on) + _engines(off)
    for k in DIRECT[1:]:
        for part in (plane, codes):
            sent += put(cores[(rank + k) % N], rank, part)
    g.wait_ge(sem.sent, sent)

    order = [(rank, None)]
    order += [((rank - k) % N, cores[(rank - k) % N]) for k in DIRECT]
    order += [((rank - k) % N, _relay_of((rank - k) % N, cores, topo)) for k in RELAYED]
    g.tensor.wait_ge(sem.qxd, 1)
    for i, (b, sender) in enumerate(order):
        if sender is None:
            g.tensor.wait_ge(sem.qwd, 1)
        else:
            g.tensor.wait_ge(sem["arr%d" % b], 2 * _engines(topo.mask(sender, core)))
        g.tensor.matmul_mx(T.ps[:, blk(b)], T.qw[:, WC * b:WC * (b + 1)], plane(b), T.qx[:], T.sx[:],
                           True, True).then_inc(sem["mm%d" % b], 1)
        if i % 2 == 0:
            g.vector.wait_ge(sem["mm%d" % b], 1)
            g.vector.tensor_copy(T.ys[:, blk(b)], T.ps[:, blk(b)]).then_inc(sem["cp%d" % b], 1)
        else:
            g.scalar.wait_ge(sem["mm%d" % b], 1)
            g.scalar.activation(T.ys[:, blk(b)], T.ps[:, blk(b)], ActivationFunctionType.Copy).then_inc(sem["cp%d" % b], 1)
        g.sync.wait_ge(sem["cp%d" % b], 1)
        g.sync.dma_start(T.y[:, blk(b)], T.ys[:, blk(b)]).then_inc(sem.stored, 16)
    g.sync.wait_ge(sem.stored, 16 * N)
